import numpy as np, ml_dtypes
CORES = [231,239,247,255,103,111,119,127]
N = 8
TK = 2048
def setup_inputs(rng):
    return {"x": rng.standard_normal((N, 128, TK), dtype=np.float32).astype(ml_dtypes.bfloat16), "w": rng.standard_normal((N, 128, N * 128), dtype=np.float32).astype(ml_dtypes.bfloat16)}
def reference(x, w):
    X, W = x.astype(np.float64), w.astype(np.float64)
    y = np.zeros((N, 128, TK))
    for r in range(N):
        for j in range(N):
            y[r] += W[r][:, 128 * j:128 * j + 128].T @ X[j]
    return {"y": y.astype(ml_dtypes.bfloat16 if x.dtype != np.float64 else np.float64)}

@@ -1,0 +1,204 @@
+from concourse.bass import DstId, RemoteDMATransfer
+from concourse.mybir import AluOpType
+
+TK, TW = 2048, 128
+C = 128
+NX = 1
+NPO, NPI = 1, 1
+LAG = 0
+NT = 2
+R = TK // C
+HALF = 4 * TW
+TL0 = NX * 4 * C
+PO0 = TL0 + NT * TW
+PI0 = PO0 + NPO * C
+TOT = PI0 + NPI * C
+
+SCRATCH = {
+    "sb": ("sbuf", [128, TOT], "bfloat16"),
+    "acc": ("psum", [128, 512], "float32"),
+    "stash": ("psum", [128, 8 * TW], "bfloat16"),
+}
+SEMAPHORES = (["wst", "wl", "wa", "st", "wo", "go", "cl", "mm", "tr", "ev", "ad"]
+              + ["ld%d" % s for s in range(NX)] + ["xl%d" % s for s in range(NX)]
+              + ["xa%d_%d" % (i, s) for i in range(4) for s in range(NX)]
+              + ["xc%d_%d" % (i, s) for i in range(4) for s in range(NX)]
+              + ["pa%d" % s for s in range(NPI)] + ["pc%d" % s for s in range(NPI)]
+              + ["pl%d" % s for s in range(NPO)] + ["ys%d" % s for s in range(NPO)])
+
+
+def rank_program(g, core, T, topo):
+    if T.rank_of(core) is None:
+        return
+    cores = list(T.cores)
+    mate = [d for d in cores if topo.mates(core, d)][0]
+    plane = [d for d in cores if d == core or topo.same_plane(core, d)]
+    mplane = [d for d in cores if d == mate or topo.same_plane(mate, d)]
+    me = plane.index(core)
+    others = [i for i in range(4) if i != me]
+    order = [me] + others
+
+    def engines(m):
+        return [1 << b for b in range(16) if (m >> b) & 1]
+
+    pmask = topo.mask(core, mate)
+    xmask = pmask
+    for i in others:
+        xmask &= topo.mask(core, plane[i])
+    nP, nX = len(engines(pmask)), len(engines(xmask))
+    one = engines(xmask & pmask)
+
+    def dst(d):
+        rid, pid = topo.addr(d, core)
+        return DstId(rid=rid, pnc=pid)
+
+    S = T.sem
+    due = {}
+
+    def inc(name, n):
+        due[name] = due.get(name, 0) + n
+        return S[name]
+
+    sb, acc, stash = T.sb, T.acc, T.stash
+    v, pe, sy, sc = g.vector, g.tensor, g.sync, g.scalar
+
+    def xb(s, i):
+        return sb[:, (s * 4 + i) * C:(s * 4 + i + 1) * C]
+
+    def tl(s):
+        return sb[:, TL0 + s * TW:TL0 + (s + 1) * TW]
+
+    def po(s):
+        return sb[:, PO0 + s * C:PO0 + (s + 1) * C]
+
+    def pi(s):
+        return sb[:, PI0 + s * C:PI0 + (s + 1) * C]
+
+    def oreg(k):
+        a = (1 + k % (LAG + 1)) * C
+        return acc[:, a:a + C]
+
+    def signal(targets):
+        g.remote_dma_fused([RemoteDMATransfer(dst_ids=[dst(d)], dma_engine_mask=one[n], remote_sem=S[name])
+                            for n, (d, name) in enumerate(targets)], local_sem=inc("cl", len(targets)))
+
+    due["wa"], due["go"] = nP, 3
+    for k in range(R):
+        for i in others:
+            inc("xa%d_%d" % (i, k % NX), nX)
+            if k + NX < R:
+                inc("xc%d_%d" % (i, k % NX), 1)
+        inc("pa%d" % (k % NPI), nP)
+        if k < NPI or k - NPI >= 0:
+            inc("pc%d" % (k % NPI), 1)
+
+    for t, d in enumerate(mplane):
+        j = T.rank_of(d)
+        (sy if t % 2 == 0 else sc).dma_start(sb[:, t * TW:(t + 1) * TW], T.w[:, j * TW:(j + 1) * TW]).then_inc(inc("wst", 16), 16)
+    g.wait_ge(S.wst, 64)
+    rid, pid = topo.addr(mate, core)
+    g.remote_dma(out_ap=sb[:, HALF:2 * HALF], in_ap=sb[:, 0:HALF], remote_sem=S.wa, local_sem=inc("wl", nP),
+                 pid=pid, routing_id=rid, dma_engine_mask=pmask)
+    g.wait_ge(S.wl, nP)
+    signal([(plane[i], "go") for i in others])
+
+    def load_x(k):
+        sy.dma_start(xb(k % NX, me), T.x[:, k * C:(k + 1) * C]).then_inc(inc("ld%d" % (k % NX), 16), 16)
+
+    sy.wait_ge(S.wl, nP)
+    for k in range(NX):
+        load_x(k)
+    v.wait_ge(S.wa, nP)
+    v.tensor_copy(stash[:, 0:HALF], sb[:, HALF:2 * HALF]).then_inc(inc("st", 1), 1)
+    sy.wait_ge(S.st, 1)
+    sc.wait_ge(S.st, 1)
+    for t, d in enumerate(plane):
+        j = T.rank_of(d)
+        (sy if t % 2 == 0 else sc).dma_start(sb[:, HALF + t * TW:HALF + (t + 1) * TW],
+                                             T.w[:, j * TW:(j + 1) * TW]).then_inc(inc("wo", 16), 16)
+    v.wait_ge(S.wo, 64)
+    v.tensor_copy(stash[:, HALF:2 * HALF], sb[:, HALF:2 * HALF]).then_inc(inc("st", 1), 1)
+    v.wait_ge(S.st, 2)
+
+    def fetch(n):
+        t = n % 8
+        col = (HALF if t < 4 else 0) + order[t % 4] * TW
+        v.tensor_copy(tl(n % NT), stash[:, col:col + TW]).then_inc(inc("tr", 1), 1)
+
+    for t in range(NT):
+        fetch(t)
+    for k in range(R + LAG):
+        if k < R:
+            for t in range(NT, 8):
+                v.wait_ge(S.mm, 8 * k + t - NT + 1)
+                fetch(8 * k + t)
+            v.wait_ge(S.mm, 8 * (k + 1))
+            if k >= NPO:
+                v.wait_ge(S["ys%d" % (k % NPO)], 16 * (k // NPO))
+            v.tensor_copy(po(k % NPO), acc[:, 0:C]).then_inc(inc("ev", 1), 1)
+            if k + 1 < R:
+                for t in range(NT):
+                    fetch(8 * (k + 1) + t)
+        j = k - LAG
+        if j >= 0:
+            v.wait_ge(S["pa%d" % (j % NPI)], nP * (j // NPI + 1))
+            v.wait_ge(S["pl%d" % (j % NPO)], nP * (j // NPO + 1))
+            v.tensor_tensor(out=po(j % NPO), in0=oreg(j), in1=pi(j % NPI), op=AluOpType.add).then_inc(inc("ad", 1), 1)
+
+    for k in range(R):
+        s, u = k % NX, k // NX + 1
+        if k > 0:
+            pe.wait_ge(S.ev, k)
+        if k - LAG > 0:
+            pe.wait_ge(S.ad, k - LAG)
+        for t in range(8):
+            i = order[t % 4]
+            if t < 4:
+                if i == me:
+                    pe.wait_ge(S["ld%d" % s], 16 * u)
+                else:
+                    pe.wait_ge(S["xa%d_%d" % (i, s)], nX * u)
+            pe.wait_ge(S.tr, 8 * k + t + 1)
+            pe.matmul(oreg(k) if t < 4 else acc[:, 0:C], lhsT=tl((8 * k + t) % NT), rhs=xb(s, i),
+                      start=(t % 4 == 0), stop=(t % 4 == 3)).then_inc(inc("mm", 1), 1)
+
+    for k in range(NX, R):
+        sy.wait_ge(S.mm, 8 * (k - NX + 1))
+        sy.wait_ge(S["xl%d" % (k % NX)], nX * (k // NX))
+        load_x(k)
+    for j in range(R):
+        sc.wait_ge(S.ad, j + 1)
+        sc.dma_start(T.y[:, j * C:(j + 1) * C], po(j % NPO)).then_inc(inc("ys%d" % (j % NPO), 16), 16)
+
+    def send_x(k):
+        s = k % NX
+        g.wait_ge(S["ld%d" % s], 16 * (k // NX + 1))
+        g.remote_dma_fused([RemoteDMATransfer(dst_ids=[dst(plane[i]) for i in others], dma_engine_mask=xmask,
+                                              remote_sem=S["xa%d_%d" % (me, s)], srcs=[xb(s, me)],
+                                              dsts=[xb(s, me) for i in others], alu_op=0)],
+                           local_sem=inc("xl%d" % s, nX))
+
+    g.wait_ge(S.go, 3)
+    for k in range(NX):
+        send_x(k)
+    g.wait_ge(S.st, 2)
+    signal([(mate, "pc%d" % s) for s in range(NPI)])
+    for k in range(R + LAG):
+        if k < R:
+            if k + NX < R:
+                g.wait_ge(S.mm, 8 * (k + 1))
+                signal([(plane[i], "xc%d_%d" % (me, k % NX)) for i in others])
+            g.wait_ge(S.ev, k + 1)
+            g.wait_ge(S["pc%d" % (k % NPI)], k // NPI + 1)
+            g.remote_dma(out_ap=pi(k % NPI), in_ap=po(k % NPO), remote_sem=S["pa%d" % (k % NPI)],
+                         local_sem=inc("pl%d" % (k % NPO), nP), pid=pid, routing_id=rid, dma_engine_mask=pmask)
+            if k + NX < R:
+                for i in others:
+                    g.wait_ge(S["xc%d_%d" % (i, k % NX)], k // NX + 1)
+                send_x(k + NX)
+        j = k - LAG
+        if j >= 0 and j + NPI < R:
+            g.wait_ge(S.ad, j + 1)
+            signal([(mate, "pc%d" % (j % NPI))])
+    for name in sorted(due):
+        g.wait_ge(S[name], due[name])

@@ -3,28 +3,20 @@ from concourse.mybir import AluOpType
 
 TK, TW = 2048, 128
 C = 128
-NX = 1
-NPO, NPI = 1, 1
-LAG = 0
-NT = 2
 R = TK // C
 HALF = 4 * TW
-TL0 = NX * 4 * C
-PO0 = TL0 + NT * TW
-PI0 = PO0 + NPO * C
-TOT = PI0 + NPI * C
+TL0 = 4 * C
+YS0 = TL0 + 2 * TW
+PI0 = YS0 + C
+TOT = PI0 + C
 
 SCRATCH = {
     "sb": ("sbuf", [128, TOT], "bfloat16"),
     "acc": ("psum", [128, 512], "float32"),
     "stash": ("psum", [128, 8 * TW], "bfloat16"),
 }
-SEMAPHORES = (["wst", "wl", "wa", "st", "wo", "go", "cl", "mm", "tr", "ev", "ad"]
-              + ["ld%d" % s for s in range(NX)] + ["xl%d" % s for s in range(NX)]
-              + ["xa%d_%d" % (i, s) for i in range(4) for s in range(NX)]
-              + ["xc%d_%d" % (i, s) for i in range(4) for s in range(NX)]
-              + ["pa%d" % s for s in range(NPI)] + ["pc%d" % s for s in range(NPI)]
-              + ["pl%d" % s for s in range(NPO)] + ["ys%d" % s for s in range(NPO)])
+SEMAPHORES = (["wst", "wl", "wa", "st", "wo", "go", "cl", "mm", "tr", "ev", "a1", "ad", "ld", "xl", "pl", "pa", "pc", "yd"]
+              + ["xa%d" % i for i in range(4)] + ["xc%d" % i for i in range(4)])
 
 
 def rank_program(g, core, T, topo):
@@ -46,7 +38,7 @@ def rank_program(g, core, T, topo):
     for i in others:
         xmask &= topo.mask(core, plane[i])
     nP, nX = len(engines(pmask)), len(engines(xmask))
-    one = engines(xmask & pmask)
+    one = engines(xmask)
 
     def dst(d):
         rid, pid = topo.addr(d, core)
@@ -62,35 +54,29 @@ def rank_program(g, core, T, topo):
     sb, acc, stash = T.sb, T.acc, T.stash
     v, pe, sy, sc = g.vector, g.tensor, g.sync, g.scalar
 
-    def xb(s, i):
-        return sb[:, (s * 4 + i) * C:(s * 4 + i + 1) * C]
+    def xb(i):
+        return sb[:, i * C:(i + 1) * C]
 
     def tl(s):
         return sb[:, TL0 + s * TW:TL0 + (s + 1) * TW]
 
-    def po(s):
-        return sb[:, PO0 + s * C:PO0 + (s + 1) * C]
+    ys, pi, mreg = sb[:, YS0:YS0 + C], sb[:, PI0:PI0 + C], acc[:, 0:C]
+    opeer = acc[:, C:2 * C]
 
-    def pi(s):
-        return sb[:, PI0 + s * C:PI0 + (s + 1) * C]
-
-    def oreg(k):
-        a = (1 + k % (LAG + 1)) * C
+    def oown(k):
+        a = (2 + k % 2) * C
         return acc[:, a:a + C]
+
+    SLOT = [0, 0, 0, 1, 0, 1, 0, 1]
+    PREV = [None, 0, 1, None, 2, 3, 4, 5]
 
     def signal(targets):
         g.remote_dma_fused([RemoteDMATransfer(dst_ids=[dst(d)], dma_engine_mask=one[n], remote_sem=S[name])
                             for n, (d, name) in enumerate(targets)], local_sem=inc("cl", len(targets)))
 
-    due["wa"], due["go"] = nP, 3
-    for k in range(R):
-        for i in others:
-            inc("xa%d_%d" % (i, k % NX), nX)
-            if k + NX < R:
-                inc("xc%d_%d" % (i, k % NX), 1)
-        inc("pa%d" % (k % NPI), nP)
-        if k < NPI or k - NPI >= 0:
-            inc("pc%d" % (k % NPI), 1)
+    due["wa"], due["go"], due["pa"], due["pc"] = nP, 3, nP * R, R
+    for i in others:
+        due["xa%d" % i], due["xc%d" % i] = nX * R, R - 1
 
     for t, d in enumerate(mplane):
         j = T.rank_of(d)
@@ -103,11 +89,10 @@ def rank_program(g, core, T, topo):
     signal([(plane[i], "go") for i in others])
 
     def load_x(k):
-        sy.dma_start(xb(k % NX, me), T.x[:, k * C:(k + 1) * C]).then_inc(inc("ld%d" % (k % NX), 16), 16)
+        sy.dma_start(xb(me), T.x[:, k * C:(k + 1) * C]).then_inc(inc("ld", 16), 16)
 
     sy.wait_ge(S.wl, nP)
-    for k in range(NX):
-        load_x(k)
+    load_x(0)
     v.wait_ge(S.wa, nP)
     v.tensor_copy(stash[:, 0:HALF], sb[:, HALF:2 * HALF]).then_inc(inc("st", 1), 1)
     sy.wait_ge(S.st, 1)
@@ -120,85 +105,77 @@ def rank_program(g, core, T, topo):
     v.tensor_copy(stash[:, HALF:2 * HALF], sb[:, HALF:2 * HALF]).then_inc(inc("st", 1), 1)
     v.wait_ge(S.st, 2)
 
-    def fetch(n):
-        t = n % 8
-        col = (HALF if t < 4 else 0) + order[t % 4] * TW
-        v.tensor_copy(tl(n % NT), stash[:, col:col + TW]).then_inc(inc("tr", 1), 1)
+    def fetch(k, t):
+        col = HALF + me * TW if t == 0 else (order[t - 1] * TW if t < 5 else HALF + order[t - 4] * TW)
+        v.tensor_copy(tl(SLOT[t]), stash[:, col:col + TW]).then_inc(inc("tr", 1), 1)
 
-    for t in range(NT):
-        fetch(t)
-    for k in range(R + LAG):
-        if k < R:
-            for t in range(NT, 8):
-                v.wait_ge(S.mm, 8 * k + t - NT + 1)
-                fetch(8 * k + t)
-            v.wait_ge(S.mm, 8 * (k + 1))
-            if k >= NPO:
-                v.wait_ge(S["ys%d" % (k % NPO)], 16 * (k // NPO))
-            v.tensor_copy(po(k % NPO), acc[:, 0:C]).then_inc(inc("ev", 1), 1)
-            if k + 1 < R:
-                for t in range(NT):
-                    fetch(8 * (k + 1) + t)
-        j = k - LAG
-        if j >= 0:
-            v.wait_ge(S["pa%d" % (j % NPI)], nP * (j // NPI + 1))
-            v.wait_ge(S["pl%d" % (j % NPO)], nP * (j // NPO + 1))
-            v.tensor_tensor(out=po(j % NPO), in0=oreg(j), in1=pi(j % NPI), op=AluOpType.add).then_inc(inc("ad", 1), 1)
+    def add(j):
+        v.wait_ge(S.pa, nP * (j + 1))
+        if j > 0:
+            v.wait_ge(S.yd, 16 * j)
+        v.tensor_tensor(out=ys, in0=oown(j), in1=pi, op=AluOpType.add).then_inc(inc("a1", 1), 1)
+        v.wait_ge(S.a1, j + 1)
+        v.tensor_tensor(out=ys, in0=opeer, in1=ys, op=AluOpType.add).then_inc(inc("ad", 1), 1)
 
     for k in range(R):
-        s, u = k % NX, k // NX + 1
-        if k > 0:
-            pe.wait_ge(S.ev, k)
-        if k - LAG > 0:
-            pe.wait_ge(S.ad, k - LAG)
         for t in range(8):
-            i = order[t % 4]
-            if t < 4:
-                if i == me:
-                    pe.wait_ge(S["ld%d" % s], 16 * u)
-                else:
-                    pe.wait_ge(S["xa%d_%d" % (i, s)], nX * u)
-            pe.wait_ge(S.tr, 8 * k + t + 1)
-            pe.matmul(oreg(k) if t < 4 else acc[:, 0:C], lhsT=tl((8 * k + t) % NT), rhs=xb(s, i),
-                      start=(t % 4 == 0), stop=(t % 4 == 3)).then_inc(inc("mm", 1), 1)
+            if PREV[t] is not None:
+                v.wait_ge(S.mm, 8 * k + PREV[t] + 1)
+            elif t == 3 and k > 0:
+                v.wait_ge(S.pl, nP * k)
+            fetch(k, t)
+            if t == 3 and k > 0:
+                add(k - 1)
+        v.wait_ge(S.mm, 8 * (k + 1))
+        v.tensor_copy(tl(1), mreg).then_inc(inc("ev", 1), 1)
+    add(R - 1)
 
-    for k in range(NX, R):
-        sy.wait_ge(S.mm, 8 * (k - NX + 1))
-        sy.wait_ge(S["xl%d" % (k % NX)], nX * (k // NX))
+    for k in range(R):
+        for t in range(8):
+            if t == 0:
+                pe.wait_ge(S.ld, 16 * (k + 1))
+                if k > 0:
+                    pe.wait_ge(S.ev, k)
+            if t == 2 and k > 0:
+                pe.wait_ge(S.ad, k)
+            i = me if t < 2 else (order[t - 1] if t < 5 else order[t - 4])
+            if 2 <= t < 5:
+                pe.wait_ge(S["xa%d" % i], nX * (k + 1))
+            pe.wait_ge(S.tr, 8 * k + t + 1)
+            pe.matmul(oown(k) if t == 0 else (mreg if t < 5 else opeer), lhsT=tl(SLOT[t]), rhs=xb(i),
+                      start=(t in (0, 1, 5)), stop=(t in (0, 4, 7))).then_inc(inc("mm", 1), 1)
+
+    for k in range(1, R):
+        sy.wait_ge(S.mm, 8 * (k - 1) + 2)
+        sy.wait_ge(S.xl, nX * k)
         load_x(k)
     for j in range(R):
         sc.wait_ge(S.ad, j + 1)
-        sc.dma_start(T.y[:, j * C:(j + 1) * C], po(j % NPO)).then_inc(inc("ys%d" % (j % NPO), 16), 16)
+        sc.dma_start(T.y[:, j * C:(j + 1) * C], ys).then_inc(inc("yd", 16), 16)
 
     def send_x(k):
-        s = k % NX
-        g.wait_ge(S["ld%d" % s], 16 * (k // NX + 1))
+        g.wait_ge(S.ld, 16 * (k + 1))
         g.remote_dma_fused([RemoteDMATransfer(dst_ids=[dst(plane[i]) for i in others], dma_engine_mask=xmask,
-                                              remote_sem=S["xa%d_%d" % (me, s)], srcs=[xb(s, me)],
-                                              dsts=[xb(s, me) for i in others], alu_op=0)],
-                           local_sem=inc("xl%d" % s, nX))
+                                              remote_sem=S["xa%d" % me], srcs=[xb(me)],
+                                              dsts=[xb(me) for i in others], alu_op=0)], local_sem=inc("xl", nX))
 
     g.wait_ge(S.go, 3)
-    for k in range(NX):
-        send_x(k)
+    send_x(0)
     g.wait_ge(S.st, 2)
-    signal([(mate, "pc%d" % s) for s in range(NPI)])
-    for k in range(R + LAG):
-        if k < R:
-            if k + NX < R:
-                g.wait_ge(S.mm, 8 * (k + 1))
-                signal([(plane[i], "xc%d_%d" % (me, k % NX)) for i in others])
-            g.wait_ge(S.ev, k + 1)
-            g.wait_ge(S["pc%d" % (k % NPI)], k // NPI + 1)
-            g.remote_dma(out_ap=pi(k % NPI), in_ap=po(k % NPO), remote_sem=S["pa%d" % (k % NPI)],
-                         local_sem=inc("pl%d" % (k % NPO), nP), pid=pid, routing_id=rid, dma_engine_mask=pmask)
-            if k + NX < R:
-                for i in others:
-                    g.wait_ge(S["xc%d_%d" % (i, k % NX)], k // NX + 1)
-                send_x(k + NX)
-        j = k - LAG
-        if j >= 0 and j + NPI < R:
-            g.wait_ge(S.ad, j + 1)
-            signal([(mate, "pc%d" % (j % NPI))])
+    signal([(mate, "pc")])
+    for k in range(R):
+        if k + 1 < R:
+            g.wait_ge(S.mm, 8 * (k + 1))
+            signal([(plane[i], "xc%d" % me) for i in others])
+        g.wait_ge(S.ev, k + 1)
+        g.wait_ge(S.pc, k + 1)
+        g.remote_dma(out_ap=pi, in_ap=tl(1), remote_sem=S.pa, local_sem=inc("pl", nP),
+                     pid=pid, routing_id=rid, dma_engine_mask=pmask)
+        if k + 1 < R:
+            for i in others:
+                g.wait_ge(S["xc%d" % i], k + 1)
+            send_x(k + 1)
+            g.wait_ge(S.a1, k + 1)
+            signal([(mate, "pc")])
     for name in sorted(due):
         g.wait_ge(S[name], due[name])

@@ -67,8 +67,9 @@ def rank_program(g, core, T, topo):
         a = (2 + k % 2) * C
         return acc[:, a:a + C]
 
-    SLOT = [0, 0, 0, 1, 0, 1, 0, 1]
-    PREV = [None, 0, 1, None, 2, 3, 4, 5]
+    SLOT = [tl(0), tl(0), tl(0), xb(me), tl(1), tl(0), tl(1), tl(0)]
+    PREV = [None, 0, 1, None, None, 2, 4, 5]
+    VSEQ = [0, 1, 2, 4, 3, 5, 6, 7]
 
     def signal(targets):
         g.remote_dma_fused([RemoteDMATransfer(dst_ids=[dst(d)], dma_engine_mask=one[n], remote_sem=S[name])
@@ -105,9 +106,12 @@ def rank_program(g, core, T, topo):
     v.tensor_copy(stash[:, HALF:2 * HALF], sb[:, HALF:2 * HALF]).then_inc(inc("st", 1), 1)
     v.wait_ge(S.st, 2)
 
+    ready = {}
+
     def fetch(k, t):
         col = HALF + me * TW if t == 0 else (order[t - 1] * TW if t < 5 else HALF + order[t - 4] * TW)
-        v.tensor_copy(tl(SLOT[t]), stash[:, col:col + TW]).then_inc(inc("tr", 1), 1)
+        v.tensor_copy(SLOT[t], stash[:, col:col + TW]).then_inc(inc("tr", 1), 1)
+        ready[8 * k + t] = due["tr"]
 
     def add(j):
         v.wait_ge(S.pa, nP * (j + 1))
@@ -118,13 +122,15 @@ def rank_program(g, core, T, topo):
         v.tensor_tensor(out=ys, in0=opeer, in1=ys, op=AluOpType.add).then_inc(inc("ad", 1), 1)
 
     for k in range(R):
-        for t in range(8):
+        for t in VSEQ:
             if PREV[t] is not None:
                 v.wait_ge(S.mm, 8 * k + PREV[t] + 1)
-            elif t == 3 and k > 0:
+            elif t == 4 and k > 0:
                 v.wait_ge(S.pl, nP * k)
+            elif t == 3:
+                v.wait_ge(S.xl, nX * (k + 1))
             fetch(k, t)
-            if t == 3 and k > 0:
+            if t == 4 and k > 0:
                 add(k - 1)
         v.wait_ge(S.mm, 8 * (k + 1))
         v.tensor_copy(tl(1), mreg).then_inc(inc("ev", 1), 1)
@@ -141,13 +147,12 @@ def rank_program(g, core, T, topo):
             i = me if t < 2 else (order[t - 1] if t < 5 else order[t - 4])
             if 2 <= t < 5:
                 pe.wait_ge(S["xa%d" % i], nX * (k + 1))
-            pe.wait_ge(S.tr, 8 * k + t + 1)
-            pe.matmul(oown(k) if t == 0 else (mreg if t < 5 else opeer), lhsT=tl(SLOT[t]), rhs=xb(i),
+            pe.wait_ge(S.tr, ready[8 * k + t])
+            pe.matmul(oown(k) if t == 0 else (mreg if t < 5 else opeer), lhsT=SLOT[t], rhs=xb(i),
                       start=(t in (0, 1, 5)), stop=(t in (0, 4, 7))).then_inc(inc("mm", 1), 1)
 
     for k in range(1, R):
-        sy.wait_ge(S.mm, 8 * (k - 1) + 2)
-        sy.wait_ge(S.xl, nX * k)
+        sy.wait_ge(S.mm, 8 * (k - 1) + 4)
         load_x(k)
     for j in range(R):
         sc.wait_ge(S.ad, j + 1)

@@ -27,8 +27,8 @@ def rank_program(g, core, T, topo):
     plane = [d for d in cores if d == core or topo.same_plane(core, d)]
     mplane = [d for d in cores if d == mate or topo.same_plane(mate, d)]
     me = plane.index(core)
-    others = [i for i in range(4) if i != me]
-    order = [me] + others
+    others = [(me + n) % 4 for n in (1, 2, 3)]
+    order = [me] + [(me - n) % 4 for n in (1, 2, 3)]
 
     def engines(m):
         return [1 << b for b in range(16) if (m >> b) & 1]

@@ -67,9 +67,9 @@ def rank_program(g, core, T, topo):
         a = (2 + k % 2) * C
         return acc[:, a:a + C]
 
-    SLOT = [tl(0), tl(0), tl(0), xb(me), tl(1), tl(0), tl(1), tl(0)]
-    PREV = [None, 0, 1, None, None, 2, 4, 5]
-    VSEQ = [0, 1, 2, 4, 3, 5, 6, 7]
+    SLOT = [tl(0), tl(0), tl(0), xb(me), tl(1), xb(me), tl(0), tl(1)]
+    PREV = [None, 0, 1, None, None, 3, 2, 4]
+    VSEQ = [0, 1, 2, 4, 3, 6, 5, 7]
 
     def signal(targets):
         g.remote_dma_fused([RemoteDMATransfer(dst_ids=[dst(d)], dma_engine_mask=one[n], remote_sem=S[name])
@@ -152,7 +152,7 @@ def rank_program(g, core, T, topo):
                       start=(t in (0, 1, 5)), stop=(t in (0, 4, 7))).then_inc(inc("mm", 1), 1)
 
     for k in range(1, R):
-        sy.wait_ge(S.mm, 8 * (k - 1) + 4)
+        sy.wait_ge(S.mm, 8 * (k - 1) + 6)
         load_x(k)
     for j in range(R):
         sc.wait_ge(S.ad, j + 1)

from concourse.bass import DstId, RemoteDMATransfer
from concourse.mybir import AluOpType

TK, TW = 2048, 128
C = 128
R = TK // C
HALF = 4 * TW
TL0 = 4 * C
YS0 = TL0 + 2 * TW
PI0 = YS0 + C
TOT = PI0 + C

SCRATCH = {
    "sb": ("sbuf", [128, TOT], "bfloat16"),
    "acc": ("psum", [128, 512], "float32"),
    "stash": ("psum", [128, 8 * TW], "bfloat16"),
}
SEMAPHORES = (["wst", "wl", "wa", "st", "wo", "go", "cl", "mm", "tr", "ev", "a1", "ad", "ld", "xl", "pl", "pa", "pc", "yd"]
              + ["xa%d" % i for i in range(4)] + ["xc%d" % i for i in range(4)])


def rank_program(g, core, T, topo):
    if T.rank_of(core) is None:
        return
    cores = list(T.cores)
    mate = [d for d in cores if topo.mates(core, d)][0]
    plane = [d for d in cores if d == core or topo.same_plane(core, d)]
    mplane = [d for d in cores if d == mate or topo.same_plane(mate, d)]
    me = plane.index(core)
    others = [(me + n) % 4 for n in (1, 2, 3)]
    order = [me] + [(me - n) % 4 for n in (1, 2, 3)]

    def engines(m):
        return [1 << b for b in range(16) if (m >> b) & 1]

    pmask = topo.mask(core, mate)
    xmask = pmask
    for i in others:
        xmask &= topo.mask(core, plane[i])
    nP, nX = len(engines(pmask)), len(engines(xmask))
    one = engines(xmask)

    def dst(d):
        rid, pid = topo.addr(d, core)
        return DstId(rid=rid, pnc=pid)

    S = T.sem
    due = {}

    def inc(name, n):
        due[name] = due.get(name, 0) + n
        return S[name]

    sb, acc, stash = T.sb, T.acc, T.stash
    v, pe, sy, sc = g.vector, g.tensor, g.sync, g.scalar

    def xb(i):
        return sb[:, i * C:(i + 1) * C]

    def tl(s):
        return sb[:, TL0 + s * TW:TL0 + (s + 1) * TW]

    ys, pi, mreg = sb[:, YS0:YS0 + C], sb[:, PI0:PI0 + C], acc[:, 0:C]
    opeer = acc[:, C:2 * C]

    def oown(k):
        a = (2 + k % 2) * C
        return acc[:, a:a + C]

    SLOT = [tl(0), tl(0), tl(0), xb(me), tl(1), xb(me), tl(0), tl(1)]
    PREV = [None, 0, 1, None, None, 3, 2, 4]
    VSEQ = [0, 1, 2, 4, 3, 6, 5, 7]

    def signal(targets):
        g.remote_dma_fused([RemoteDMATransfer(dst_ids=[dst(d)], dma_engine_mask=one[n], remote_sem=S[name])
                            for n, (d, name) in enumerate(targets)], local_sem=inc("cl", len(targets)))

    due["wa"], due["go"], due["pa"], due["pc"] = nP, 3, nP * R, R
    for i in others:
        due["xa%d" % i], due["xc%d" % i] = nX * R, R - 1

    for t, d in enumerate(mplane):
        j = T.rank_of(d)
        (sy if t % 2 == 0 else sc).dma_start(sb[:, t * TW:(t + 1) * TW], T.w[:, j * TW:(j + 1) * TW]).then_inc(inc("wst", 16), 16)
    g.wait_ge(S.wst, 64)
    rid, pid = topo.addr(mate, core)
    g.remote_dma(out_ap=sb[:, HALF:2 * HALF], in_ap=sb[:, 0:HALF], remote_sem=S.wa, local_sem=inc("wl", nP),
                 pid=pid, routing_id=rid, dma_engine_mask=pmask)
    g.wait_ge(S.wl, nP)
    signal([(plane[i], "go") for i in others])

    def load_x(k):
        sy.dma_start(xb(me), T.x[:, k * C:(k + 1) * C]).then_inc(inc("ld", 16), 16)

    sy.wait_ge(S.wl, nP)
    load_x(0)
    v.wait_ge(S.wa, nP)
    v.tensor_copy(stash[:, 0:HALF], sb[:, HALF:2 * HALF]).then_inc(inc("st", 1), 1)
    sy.wait_ge(S.st, 1)
    sc.wait_ge(S.st, 1)
    for t, d in enumerate(plane):
        j = T.rank_of(d)
        (sy if t % 2 == 0 else sc).dma_start(sb[:, HALF + t * TW:HALF + (t + 1) * TW],
                                             T.w[:, j * TW:(j + 1) * TW]).then_inc(inc("wo", 16), 16)
    v.wait_ge(S.wo, 64)
    v.tensor_copy(stash[:, HALF:2 * HALF], sb[:, HALF:2 * HALF]).then_inc(inc("st", 1), 1)
    v.wait_ge(S.st, 2)

    ready = {}

    def fetch(k, t):
        col = HALF + me * TW if t == 0 else (order[t - 1] * TW if t < 5 else HALF + order[t - 4] * TW)
        v.tensor_copy(SLOT[t], stash[:, col:col + TW]).then_inc(inc("tr", 1), 1)
        ready[8 * k + t] = due["tr"]

    def add(j):
        v.wait_ge(S.pa, nP * (j + 1))
        if j > 0:
            v.wait_ge(S.yd, 16 * j)
        v.tensor_tensor(out=ys, in0=oown(j), in1=pi, op=AluOpType.add).then_inc(inc("a1", 1), 1)
        v.wait_ge(S.a1, j + 1)
        v.tensor_tensor(out=ys, in0=opeer, in1=ys, op=AluOpType.add).then_inc(inc("ad", 1), 1)

    for k in range(R):
        for t in VSEQ:
            if PREV[t] is not None:
                v.wait_ge(S.mm, 8 * k + PREV[t] + 1)
            elif t == 4 and k > 0:
                v.wait_ge(S.pl, nP * k)
            elif t == 3:
                v.wait_ge(S.xl, nX * (k + 1))
            fetch(k, t)
            if t == 4 and k > 0:
                add(k - 1)
        v.wait_ge(S.mm, 8 * (k + 1))
        v.tensor_copy(tl(1), mreg).then_inc(inc("ev", 1), 1)
    add(R - 1)

    for k in range(R):
        for t in range(8):
            if t == 0:
                pe.wait_ge(S.ld, 16 * (k + 1))
                if k > 0:
                    pe.wait_ge(S.ev, k)
            if t == 2 and k > 0:
                pe.wait_ge(S.ad, k)
            i = me if t < 2 else (order[t - 1] if t < 5 else order[t - 4])
            if 2 <= t < 5:
                pe.wait_ge(S["xa%d" % i], nX * (k + 1))
            pe.wait_ge(S.tr, ready[8 * k + t])
            pe.matmul(oown(k) if t == 0 else (mreg if t < 5 else opeer), lhsT=SLOT[t], rhs=xb(i),
                      start=(t in (0, 1, 5)), stop=(t in (0, 4, 7))).then_inc(inc("mm", 1), 1)

    for k in range(1, R):
        sy.wait_ge(S.mm, 8 * (k - 1) + 6)
        load_x(k)
    for j in range(R):
        sc.wait_ge(S.ad, j + 1)
        sc.dma_start(T.y[:, j * C:(j + 1) * C], ys).then_inc(inc("yd", 16), 16)

    def send_x(k):
        g.wait_ge(S.ld, 16 * (k + 1))
        g.remote_dma_fused([RemoteDMATransfer(dst_ids=[dst(plane[i]) for i in others], dma_engine_mask=xmask,
                                              remote_sem=S["xa%d" % me], srcs=[xb(me)],
                                              dsts=[xb(me) for i in others], alu_op=0)], local_sem=inc("xl", nX))

    g.wait_ge(S.go, 3)
    send_x(0)
    g.wait_ge(S.st, 2)
    signal([(mate, "pc")])
    for k in range(R):
        if k + 1 < R:
            g.wait_ge(S.mm, 8 * (k + 1))
            signal([(plane[i], "xc%d" % me) for i in others])
        g.wait_ge(S.ev, k + 1)
        g.wait_ge(S.pc, k + 1)
        g.remote_dma(out_ap=pi, in_ap=tl(1), remote_sem=S.pa, local_sem=inc("pl", nP),
                     pid=pid, routing_id=rid, dma_engine_mask=pmask)
        if k + 1 < R:
            for i in others:
                g.wait_ge(S["xc%d" % i], k + 1)
            send_x(k + 1)
            g.wait_ge(S.a1, k + 1)
            signal([(mate, "pc")])
    for name in sorted(due):
        g.wait_ge(S[name], due[name])
